import numpy as np
import ml_dtypes


def mxq(x, axis, fmt="e4m3"):
    dtype, down = {"e4m3": (ml_dtypes.float8_e4m3fn, 7), "e5m2": (ml_dtypes.float8_e5m2, 14)}[fmt]
    v = np.moveaxis(np.asarray(x, np.float32).astype(ml_dtypes.bfloat16).astype(np.float64), axis, -1)
    blocks = v.reshape(v.shape[:-1] + (-1, 32))
    amax = np.abs(blocks).max(-1, keepdims=True)
    byte = np.maximum(np.where(amax > 0, np.frexp(amax)[1] - 1 + 127, 0) - down, 1)
    scale = np.exp2(byte - 127.0)
    codes = (blocks / scale).astype(np.float32).astype(dtype).astype(np.float64)
    return np.moveaxis((codes * scale).reshape(v.shape), -1, axis)


WIDE = False


def mx_kscale(k):
    if not WIDE:
        return np.ones(k)
    levels = np.array([10, -10, 5, -5, 0])
    if k % 512:
        return np.exp2(np.random.permutation(np.resize(levels, k // 32))).repeat(32)
    a = np.empty((k // 512, 16))
    for p in range(k // 512):
        a[p, :8] = np.random.permutation(np.resize(levels, 8))
        for g in range(8):
            far = levels[np.abs(levels - a[p, g]) >= 10]
            a[p, g + 8] = far[np.random.randint(len(far))]
    return np.exp2(a.ravel()).repeat(32)


def f64(x):
    return np.asarray(x).astype(np.float64)


def striped(idx):
    return np.tile(idx.reshape(-1, 16).T, (8, 1)).astype(np.uint16)


def unstriped(offs):
    return offs[:16].T.reshape(-1).astype(np.int64)


E2M1 = np.array([0.0, 0.5, 1.0, 1.5, 2.0, 3.0, 4.0, 6.0, -0.0, -0.5, -1.0, -1.5, -2.0, -3.0, -4.0, -6.0])


def pack_weight(w, fmt):
    k, n = w.shape
    w = f64(np.asarray(w, np.float32).astype(ml_dtypes.bfloat16)).reshape(k // 32, 32, n)
    amax = np.abs(w).max(1)
    if fmt == "e4m3":
        byte = np.frexp(amax)[1] - 1 + 127 - 7
    else:
        mant, ex = np.frexp(amax / 6.0)
        byte = np.where(mant > 0.5, ex, ex - 1) + 127
    byte = np.clip(np.where(amax > 0, byte, 1), 1, 254)
    scaled = (w * np.exp2(127.0 - byte)[:, None, :]).reshape(k, n).astype(np.float32)
    by_word = np.ascontiguousarray(scaled.reshape(k // 512, 128, 4, n).transpose(0, 1, 3, 2))
    if fmt == "e4m3":
        words = by_word.astype(ml_dtypes.float8_e4m3fn).view(np.uint8)
    else:
        c = by_word.astype(ml_dtypes.float4_e2m1fn).view(np.uint8) & 0xF
        words = (c[..., 0::2] | (c[..., 1::2] << 4)).reshape(k // 512, 128, 2 * n)
    return np.ascontiguousarray(words), np.ascontiguousarray(byte.astype(np.uint8).reshape(k // 512, 16, n))


def unpack_weight(words, scales, fmt):
    g, _, n = scales.shape
    words = np.ascontiguousarray(words).reshape(g, 128, n, -1)
    if fmt == "e4m3":
        vals = words.view(ml_dtypes.float8_e4m3fn).astype(np.float64)
    else:
        nib = np.empty((g, 128, n, 4), np.uint8)
        nib[..., 0::2] = words & 0xF
        nib[..., 1::2] = words >> 4
        vals = E2M1[nib]
    vals = vals * np.repeat(np.exp2(scales.astype(np.float64) - 127.0), 8, axis=1)[..., None]
    return vals.transpose(0, 1, 3, 2).reshape(g * 512, n)


def gelu(v):
    return 0.5 * v * (1.0 + np.tanh(np.sqrt(2.0 / np.pi) * (v + 0.044715 * v**3)))


K, T, S, H, P, N, P2 = 1536, 4096, 1024, 1024, 512, 768, 256

def setup_inputs():
    n = np.random.standard_normal
    s = mx_kscale(K)[:, None]
    u = mx_kscale(H)[:, None]
    tab_words, tab_scales = pack_weight(n((K, T)) * s, "e4m3")
    w4_words, w4_scales = pack_weight(1.2 * n((H, N)) / np.sqrt(H) / u, "e2m1")
    return {
        "tab_words": tab_words, "tab_scales": tab_scales,
        "offs": striped(np.random.permutation(T)[:S]),
        "pos1": striped(np.random.permutation(S)[:P]),
        "pos2": striped(np.random.permutation(S)[:P]),
        "pos3": striped(np.random.permutation(P)[:P2]),
        "pos4": striped(np.random.permutation(P)[:P2]),
        "w1": (1.2 * n((K, H)) / np.sqrt(K) / s).astype(np.float32),
        "b1": (0.8 * n(H)).astype(np.float32),
        "depth": (np.exp(0.4 * n((H, S))) * u).astype(np.float32),
        "w4_words": w4_words, "w4_scales": w4_scales,
        "plots": np.exp(0.4 * n((N, P2))).astype(np.float32),
    }

def reference(tab_words, tab_scales, offs, pos1, pos2, pos3, pos4, w1, b1, depth, w4_words, w4_scales, plots):
    v = unpack_weight(tab_words, tab_scales, "e4m3")[:, unstriped(offs)]
    lin = (mxq(f64(w1), 0, "e4m3").T @ v) + f64(b1)[:, None]
    h = np.tanh(lin) * f64(depth)
    z = np.maximum(h[:, unstriped(pos1)], h[:, unstriped(pos2)])
    w4 = unpack_weight(w4_words, w4_scales, "e2m1")
    y = w4.T @ mxq(z, 0, "e4m3")
    gap = np.abs(y[:, unstriped(pos3)] - y[:, unstriped(pos4)])
    return gap * f64(plots)

@@ -1,0 +1,219 @@
+from contextlib import ExitStack
+
+import concourse.mybir as mybir
+
+K, T, S, H, M, N, J = 1536, 4096, 1024, 1024, 512, 768, 256
+FLOPS = 2 * K * H * S + 2 * H * N * M
+
+F32 = mybir.dt.float32
+BF16 = mybir.dt.bfloat16
+I32 = mybir.dt.int32
+U32 = mybir.dt.uint32
+U16 = mybir.dt.uint16
+U8 = mybir.dt.uint8
+FP8X4 = mybir.dt.float8_e4m3fn_x4
+FP4X4 = mybir.dt.float4_e2m1fn_x4
+ALU = mybir.AluOpType
+ACT = mybir.ActivationFunctionType
+
+P = 128
+PACK = 4
+PASS = P * PACK
+BANK = 512
+K_PASSES = K // PASS
+H_PASSES = H // PASS
+N_TILES = N // P
+HALVES = S // BANK
+
+
+def tile_list_bog_dam_contrast_kernel(
+    tc, tab_words, tab_scales, offs, pos1, pos2, pos3, pos4, w1, b1, depth, w4_words, w4_scales, plots, out
+):
+    nc = tc.nc
+    with ExitStack() as ctx:
+        keep = ctx.enter_context(tc.tile_pool(name="keep", bufs=1))
+        ring = ctx.enter_context(tc.tile_pool(name="ring", bufs=1))
+        psum = ctx.enter_context(tc.psum_pool(name="psum", bufs=1))
+
+        def load_list(ap, name):
+            tile = keep.tile([P, ap.shape[1]], U16, name=name)
+            nc.sync.dma_start(tile[:], ap)
+            return tile
+
+        def load_w1(b, a):
+            raw = ring.tile([P, PACK, PASS], F32, name="w1_raw", tag="w1_raw", bufs=4)
+            rows = w1[a * PASS : (a + 1) * PASS, b * PASS : (b + 1) * PASS]
+            nc.sync.dma_start(raw[:], rows.rearrange("(p j) c -> p j c", j=PACK))
+            return raw
+
+        def load_table(a):
+            tile = keep.tile([P, T], I32, name="table%d" % a)
+            nc.sync.dma_start(tile[:], tab_words[a].rearrange("p t i -> p (t i)").bitcast(I32))
+            return tile
+
+        def load_depth(b, t):
+            tile = keep.tile([P, S], F32, name="depth%d%d" % (b, t))
+            rows = depth[b * PASS : (b + 1) * PASS, :].rearrange("(p t) j -> p t j", t=PACK)
+            nc.sync.dma_start(tile[:], rows[:, t, :])
+            return tile
+
+        def round_w1(raw):
+            rounded = ring.tile([P, PACK * PASS], BF16, name="w1_bf16", tag="w1_bf16", bufs=2, align_bytes=64)
+            nc.scalar.copy(
+                rounded[:].rearrange("p (t m j) -> p m j t", t=PACK, j=PACK),
+                raw[:].rearrange("p j (m t) -> p m j t", t=PACK),
+            )
+            return rounded
+
+        def quantize(values, name):
+            codes = keep.tile([P, PASS], U32, name=name + "_codes", align_bytes=64)
+            scales = keep.tile([P, PASS], U8, name=name + "_scales", align_bytes=64)
+            nc.vector.quantize_mx(out=codes[:].bitcast(FP8X4), scales=scales[:], in_=values[:])
+            return codes, scales
+
+        def bank_tile(i):
+            return psum.tile([P, BANK], F32, name="bank%d" % i, tag="bank%d" % i)
+
+        table_scales = keep.tile([P, T], U8, name="table_scales")
+        nc.vector.memset(table_scales[:].bitcast(I32), 0)
+        for q in range(4):
+            nc.gpsimd.dma_start(
+                table_scales[32 * q : 32 * q + 4 * K_PASSES, :].bitcast(I32),
+                tab_scales[:, 4 * q : 4 * q + 4, :].bitcast(I32),
+            )
+        bias = keep.tile([P, H_PASSES, PACK], F32, name="bias")
+        nc.gpsimd.dma_start(bias[:], b1.rearrange("(b p t) -> p b t", b=H_PASSES, t=PACK))
+        w4_planes = keep.tile([P, H_PASSES, N], U8, name="w4_planes", align_bytes=64)
+        nc.vector.memset(w4_planes[:].bitcast(I32), 0)
+        for q in range(4):
+            nc.gpsimd.dma_start(
+                w4_planes[32 * q : 32 * q + 4, :, :].bitcast(I32),
+                w4_scales[:, 4 * q : 4 * q + 4, :].rearrange("a r c -> r a c").bitcast(I32),
+            )
+
+        w1_raw = {}
+        table = []
+        depth_sb = {}
+        w1_raw[0, 0] = load_w1(0, 0)
+        offs_sb = load_list(offs, "offs_sb")
+        for a in range(K_PASSES):
+            table.append(load_table(a))
+            if a + 1 < K_PASSES:
+                w1_raw[0, a + 1] = load_w1(0, a + 1)
+        depth_sb[0, 0] = load_depth(0, 0)
+        pos1_sb = load_list(pos1, "pos1_sb")
+        pos2_sb = load_list(pos2, "pos2_sb")
+
+        picked_scales = keep.tile([P, S], U8, name="picked_scales", align_bytes=64)
+        picked = [keep.tile([P, S], U32, name="picked%d" % a, align_bytes=64) for a in range(K_PASSES)]
+
+        def pick_words(a, lo, hi):
+            nc.vector.tensor_copy(
+                picked[a][:, lo:hi], table[a][:].bitcast(U32).indirect(offs_sb[:, lo // 16 : hi // 16])
+            )
+
+        def first_product(banks, w1_q, a, t, half):
+            codes, scales = w1_q
+            cols = slice(half * BANK, (half + 1) * BANK)
+            nc.tensor.matmul_mx(
+                out=banks[t * HALVES + half][:],
+                lhsT=codes[:, t * P : (t + 1) * P].bitcast(FP8X4),
+                lhsT_scale=scales[:, t * P : (t + 1) * P],
+                rhs=picked[a][:, cols].bitcast(FP8X4),
+                rhs_scale=picked_scales[4 * a : P, cols],
+                start=(a == 0),
+                stop=(a == K_PASSES - 1),
+            )
+
+        def features(banks, b, t):
+            h = ring.tile([P, S], F32, name="h", tag="h", bufs=5)
+            engine = nc.vector if t == 0 else nc.gpsimd
+            for half in range(HALVES):
+                cols = slice(half * BANK, (half + 1) * BANK)
+                nc.scalar.activation(h[:, cols], banks[t * HALVES + half][:], ACT.Tanh, bias=bias[:, b, t : t + 1])
+                engine.tensor_tensor(h[:, cols], h[:, cols], depth_sb[b, t][:, cols], ALU.mult)
+            return h
+
+        def dam_maxima(hs, name):
+            above = ring.tile([P, PACK, M], F32, name="above", tag="above")
+            below = ring.tile([P, PACK, M], F32, name="below", tag="below")
+            for t in range(PACK):
+                nc.vector.tensor_copy(above[:, t, :], hs[t][:].indirect(pos1_sb[:]))
+                nc.vector.tensor_copy(below[:, t, :], hs[t][:].indirect(pos2_sb[:]))
+            z = ring.tile([P, PACK * M], BF16, name="z", tag="z", bufs=2, align_bytes=64)
+            nc.vector.tensor_tensor(
+                z[:].rearrange("p (c i t) -> p c t i", i=4, t=PACK),
+                above[:].rearrange("p t (c i) -> p c t i", i=4),
+                below[:].rearrange("p t (c i) -> p c t i", i=4),
+                ALU.max,
+            )
+            return quantize(z, name)
+
+        nc.vector.tensor_copy(picked_scales[:], table_scales[:].indirect(offs_sb[:]))
+        banks = [bank_tile(i) for i in range(PACK * HALVES)]
+        for a in range(K_PASSES):
+            w1_q = quantize(round_w1(w1_raw[0, a]), "w1_0%d" % a)
+            if a + 1 < K_PASSES:
+                pick_words(a, 0, S)
+            else:
+                for half in range(HALVES):
+                    pick_words(a, half * BANK, (half + 1) * BANK)
+            for t in range(PACK):
+                for half in range(HALVES):
+                    first_product(banks, w1_q, a, t, half)
+
+        for a in range(K_PASSES):
+            depth_sb[0, a + 1] = load_depth(0, a + 1)
+            w1_raw[1, a] = load_w1(1, a)
+        depth_sb[1, 0] = load_depth(1, 0)
+        w4_sb = keep.tile([P, H_PASSES, 2 * N], U8, name="w4_sb", align_bytes=64)
+        nc.sync.dma_start(w4_sb[:].bitcast(I32), w4_words.rearrange("a p c -> p a c").bitcast(I32))
+        for t in range(1, PACK):
+            depth_sb[1, t] = load_depth(1, t)
+        pos3_sb = load_list(pos3, "pos3_sb")
+        pos4_sb = load_list(pos4, "pos4_sb")
+        plots_sb = keep.tile([P, N_TILES, J], F32, name="plots_sb")
+        nc.sync.dma_start(plots_sb[:], plots.rearrange("(n p) j -> p n j", p=P))
+
+        hs0 = [features(banks, 0, t) for t in range(PACK)]
+
+        banks = [bank_tile(i) for i in range(PACK * HALVES)]
+        for a in range(K_PASSES):
+            w1_q = quantize(round_w1(w1_raw[1, a]), "w1_1%d" % a)
+            for t in range(PACK):
+                for half in range(HALVES):
+                    first_product(banks, w1_q, a, t, half)
+        z_q = [dam_maxima(hs0, "z0")]
+        hs1 = [features(banks, 1, t) for t in range(PACK)]
+        z_q.append(dam_maxima(hs1, "z1"))
+
+        def second_product(n):
+            bank = bank_tile(n)
+            for b in range(H_PASSES):
+                codes, scales = z_q[b]
+                nc.tensor.matmul_mx(
+                    out=bank[:],
+                    lhsT=w4_sb[:, b, 2 * n * P : 2 * (n + 1) * P].bitcast(FP4X4),
+                    lhsT_scale=w4_planes[:, b, n * P : (n + 1) * P],
+                    rhs=codes[:].bitcast(FP8X4),
+                    rhs_scale=scales[:],
+                    start=(b == 0),
+                    stop=(b == H_PASSES - 1),
+                )
+            y = keep.tile([P, M], F32, name="y%d" % n)
+            nc.scalar.copy(y[:], bank[:])
+            return y
+
+        ahead = 2
+        ys = [second_product(n) for n in range(ahead)]
+        for n in range(N_TILES):
+            if n + ahead < N_TILES:
+                ys.append(second_product(n + ahead))
+            one = ring.tile([P, J], F32, name="one", tag="one", bufs=2)
+            nc.vector.tensor_copy(one[:], ys[n][:].indirect(pos3_sb[:]))
+            gap = ring.tile([P, J], F32, name="gap", tag="gap", bufs=2)
+            nc.vector.tensor_tensor(gap[:], ys[n][:].indirect(pos4_sb[:]), one[:], ALU.subtract)
+            nc.scalar.activation(gap[:], gap[:], ACT.Abs)
+            result = ring.tile([P, J], F32, name="result", tag="result", bufs=N_TILES)
+            nc.vector.tensor_tensor(result[:], gap[:], plots_sb[:, n, :], ALU.mult)
+            nc.sync.dma_start(out[n * P : (n + 1) * P, :], result[:])

@@ -21,9 +21,9 @@ PACK = 4
 PASS = P * PACK
 BANK = 512
 K_PASSES = K // PASS
-H_PASSES = H // PASS
 N_TILES = N // P
 HALVES = S // BANK
+GROUPS = ((0, 2), (256, 2), (512, 4))
 
 
 def tile_list_bog_dam_contrast_kernel(
@@ -40,50 +40,72 @@ def tile_list_bog_dam_contrast_kernel(
             nc.sync.dma_start(tile[:], ap)
             return tile
 
-        def load_w1(b, a):
-            raw = ring.tile([P, PACK, PASS], F32, name="w1_raw", tag="w1_raw", bufs=4)
-            rows = w1[a * PASS : (a + 1) * PASS, b * PASS : (b + 1) * PASS]
+        def load_w1(g, a):
+            first, tiles = GROUPS[g]
+            if tiles == PACK:
+                raw = ring.tile([P, PACK, tiles * P], F32, name="w1_wide", tag="big", bufs=K_PASSES)
+            else:
+                raw = ring.tile([P, PACK, tiles * P], F32, name="w1_raw", tag="w1_raw", bufs=4)
+            rows = w1[a * PASS : (a + 1) * PASS, first : first + tiles * P]
             nc.sync.dma_start(raw[:], rows.rearrange("(p j) c -> p j c", j=PACK))
             return raw
 
         def load_table(a):
-            tile = keep.tile([P, T], I32, name="table%d" % a)
+            tile = ring.tile([P, T], I32, name="table", tag="big", bufs=K_PASSES)
             nc.sync.dma_start(tile[:], tab_words[a].rearrange("p t i -> p (t i)").bitcast(I32))
             return tile
 
-        def load_depth(b, t):
-            tile = keep.tile([P, S], F32, name="depth%d%d" % (b, t))
-            rows = depth[b * PASS : (b + 1) * PASS, :].rearrange("(p t) j -> p t j", t=PACK)
-            nc.sync.dma_start(tile[:], rows[:, t, :])
+        def load_depth(g, s):
+            first, tiles = GROUPS[g]
+            tile = ring.tile([P, S], F32, name="depth_sb", tag="depth_sb", bufs=6, align_bytes=64)
+            rows = depth[first : first + tiles * P, :].rearrange("(p s) j -> p s j", s=tiles)
+            nc.sync.dma_start(tile[:], rows[:, s, :])
             return tile
 
-        def round_w1(raw):
-            rounded = ring.tile([P, PACK * PASS], BF16, name="w1_bf16", tag="w1_bf16", bufs=2, align_bytes=64)
+        def round_w1(g, a, raw):
+            tiles = GROUPS[g][1]
+            if (g, a) in reused:
+                rounded = reused[g, a][:].bitcast(BF16)
+            else:
+                tile = ring.tile([P, tiles * PASS], BF16, name="w1_bf16", tag="w1_bf16", bufs=2, align_bytes=64)
+                rounded = tile[:]
+            pair = PACK // tiles
             nc.scalar.copy(
-                rounded[:].rearrange("p (t m j) -> p m j t", t=PACK, j=PACK),
-                raw[:].rearrange("p j (m t) -> p m j t", t=PACK),
+                rounded.rearrange("p (s c i j) -> p c j i s", s=tiles, i=pair, j=PACK),
+                raw[:].rearrange("p j (c i s) -> p c j i s", s=tiles, i=pair),
             )
             return rounded
 
-        def quantize(values, name):
-            codes = keep.tile([P, PASS], U32, name=name + "_codes", align_bytes=64)
-            scales = keep.tile([P, PASS], U8, name=name + "_scales", align_bytes=64)
-            nc.vector.quantize_mx(out=codes[:].bitcast(FP8X4), scales=scales[:], in_=values[:])
+        def quantize(values, width, name):
+            codes = keep.tile([P, width], U32, name=name + "_codes", align_bytes=64)
+            scales = keep.tile([P, width], U8, name=name + "_scales", align_bytes=64)
+            nc.vector.quantize_mx(out=codes[:].bitcast(FP8X4), scales=scales[:], in_=values)
             return codes, scales
 
         def bank_tile(i):
             return psum.tile([P, BANK], F32, name="bank%d" % i, tag="bank%d" % i)
 
+        reused = {
+            (g, a): keep.tile([P, GROUPS[g][1] * PASS // 2], F32, name="reused%d%d" % (g, a), align_bytes=64)
+            for g, a in ((1, 1), (1, 2), (2, 0), (2, 1), (2, 2))
+        }
+        w1_raw = {}
+        table = []
+        depth_sb = {}
         table_scales = keep.tile([P, T], U8, name="table_scales")
         nc.vector.memset(table_scales[:].bitcast(I32), 0)
+        table.append(load_table(0))
         for q in range(4):
             nc.gpsimd.dma_start(
                 table_scales[32 * q : 32 * q + 4 * K_PASSES, :].bitcast(I32),
                 tab_scales[:, 4 * q : 4 * q + 4, :].bitcast(I32),
             )
-        bias = keep.tile([P, H_PASSES, PACK], F32, name="bias")
-        nc.gpsimd.dma_start(bias[:], b1.rearrange("(b p t) -> p b t", b=H_PASSES, t=PACK))
-        w4_planes = keep.tile([P, H_PASSES, N], U8, name="w4_planes", align_bytes=64)
+        bias = []
+        for g, (first, tiles) in enumerate(GROUPS):
+            tile = keep.tile([P, tiles], F32, name="bias%d" % g)
+            nc.gpsimd.dma_start(tile[:], b1[first : first + tiles * P].rearrange("(p s) -> p s", s=tiles))
+            bias.append(tile)
+        w4_planes = keep.tile([P, 2, N], U8, name="w4_planes", align_bytes=64)
         nc.vector.memset(w4_planes[:].bitcast(I32), 0)
         for q in range(4):
             nc.gpsimd.dma_start(
@@ -91,15 +113,13 @@ def tile_list_bog_dam_contrast_kernel(
                 w4_scales[:, 4 * q : 4 * q + 4, :].rearrange("a r c -> r a c").bitcast(I32),
             )
 
-        w1_raw = {}
-        table = []
-        depth_sb = {}
-        w1_raw[0, 0] = load_w1(0, 0)
         offs_sb = load_list(offs, "offs_sb")
-        for a in range(K_PASSES):
-            table.append(load_table(a))
-            if a + 1 < K_PASSES:
-                w1_raw[0, a + 1] = load_w1(0, a + 1)
+        w1_raw[0, 0] = load_w1(0, 0)
+        table.append(load_table(1))
+        w1_raw[0, 1] = load_w1(0, 1)
+        w1_raw[0, 2] = load_w1(0, 2)
+        table.append(load_table(2))
+        w1_raw[1, 0] = load_w1(1, 0)
         depth_sb[0, 0] = load_depth(0, 0)
         pos1_sb = load_list(pos1, "pos1_sb")
         pos2_sb = load_list(pos2, "pos2_sb")
@@ -112,93 +132,148 @@ def tile_list_bog_dam_contrast_kernel(
                 picked[a][:, lo:hi], table[a][:].bitcast(U32).indirect(offs_sb[:, lo // 16 : hi // 16])
             )
 
-        def first_product(banks, w1_q, a, t, half):
-            codes, scales = w1_q
-            cols = slice(half * BANK, (half + 1) * BANK)
-            nc.tensor.matmul_mx(
-                out=banks[t * HALVES + half][:],
-                lhsT=codes[:, t * P : (t + 1) * P].bitcast(FP8X4),
-                lhsT_scale=scales[:, t * P : (t + 1) * P],
-                rhs=picked[a][:, cols].bitcast(FP8X4),
-                rhs_scale=picked_scales[4 * a : P, cols],
-                start=(a == 0),
-                stop=(a == K_PASSES - 1),
-            )
+        def first_pass(g, a, banks):
+            tiles = GROUPS[g][1]
+            codes, scales = quantize(round_w1(g, a, w1_raw[g, a]), tiles * P, "w1_%d%d" % (g, a))
+            if g == 0:
+                pieces = HALVES if a == K_PASSES - 1 else 1
+                for piece in range(pieces):
+                    pick_words(a, piece * S // pieces, (piece + 1) * S // pieces)
+            for s in range(tiles):
+                for half in range(HALVES):
+                    cols = slice(half * BANK, (half + 1) * BANK)
+                    nc.tensor.matmul_mx(
+                        out=banks[s * HALVES + half][:],
+                        lhsT=codes[:, s * P : (s + 1) * P].bitcast(FP8X4),
+                        lhsT_scale=scales[:, s * P : (s + 1) * P],
+                        rhs=picked[a][:, cols].bitcast(FP8X4),
+                        rhs_scale=picked_scales[4 * a : P, cols],
+                        start=(a == 0),
+                        stop=(a == K_PASSES - 1),
+                    )
 
-        def features(banks, b, t):
-            h = ring.tile([P, S], F32, name="h", tag="h", bufs=5)
-            engine = nc.vector if t == 0 else nc.gpsimd
+        def bounded(g, s):
+            h = ring.tile([P, S], F32, name="h", tag="h", bufs=4)
             for half in range(HALVES):
                 cols = slice(half * BANK, (half + 1) * BANK)
-                nc.scalar.activation(h[:, cols], banks[t * HALVES + half][:], ACT.Tanh, bias=bias[:, b, t : t + 1])
-                engine.tensor_tensor(h[:, cols], h[:, cols], depth_sb[b, t][:, cols], ALU.mult)
+                nc.scalar.activation(h[:, cols], banks[g][s * HALVES + half][:], ACT.Tanh, bias=bias[g][:, s : s + 1])
             return h
 
-        def dam_maxima(hs, name):
-            above = ring.tile([P, PACK, M], F32, name="above", tag="above")
-            below = ring.tile([P, PACK, M], F32, name="below", tag="below")
-            for t in range(PACK):
-                nc.vector.tensor_copy(above[:, t, :], hs[t][:].indirect(pos1_sb[:]))
-                nc.vector.tensor_copy(below[:, t, :], hs[t][:].indirect(pos2_sb[:]))
-            z = ring.tile([P, PACK * M], BF16, name="z", tag="z", bufs=2, align_bytes=64)
-            nc.vector.tensor_tensor(
-                z[:].rearrange("p (c i t) -> p c t i", i=4, t=PACK),
-                above[:].rearrange("p t (c i) -> p c t i", i=4),
-                below[:].rearrange("p t (c i) -> p c t i", i=4),
-                ALU.max,
-            )
-            return quantize(z, name)
+        def times_depth(g, s, h):
+            pieces = HALVES if (g, s) == (0, 0) else 1
+            for piece in range(pieces):
+                cols = slice(piece * S // pieces, (piece + 1) * S // pieces)
+                nc.vector.tensor_tensor(h[:, cols], h[:, cols], depth_sb[g, s][:, cols], ALU.mult)
+
+        def pick_dams(h, above, below):
+            nc.vector.tensor_copy(above, h[:].indirect(pos1_sb[:]))
+            nc.vector.tensor_copy(below, h[:].indirect(pos2_sb[:]))
 
         nc.vector.tensor_copy(picked_scales[:], table_scales[:].indirect(offs_sb[:]))
-        banks = [bank_tile(i) for i in range(PACK * HALVES)]
+        banks = {0: [bank_tile(i) for i in range(4)]}
         for a in range(K_PASSES):
-            w1_q = quantize(round_w1(w1_raw[0, a]), "w1_0%d" % a)
-            if a + 1 < K_PASSES:
-                pick_words(a, 0, S)
-            else:
-                for half in range(HALVES):
-                    pick_words(a, half * BANK, (half + 1) * BANK)
-            for t in range(PACK):
-                for half in range(HALVES):
-                    first_product(banks, w1_q, a, t, half)
+            first_pass(0, a, banks[0])
 
-        for a in range(K_PASSES):
-            depth_sb[0, a + 1] = load_depth(0, a + 1)
-            w1_raw[1, a] = load_w1(1, a)
+        w1_raw[1, 1] = load_w1(1, 1)
+        w1_raw[1, 2] = load_w1(1, 2)
+        depth_sb[0, 1] = load_depth(0, 1)
+        w1_raw[2, 0] = load_w1(2, 0)
         depth_sb[1, 0] = load_depth(1, 0)
-        w4_sb = keep.tile([P, H_PASSES, 2 * N], U8, name="w4_sb", align_bytes=64)
+        w1_raw[2, 1] = load_w1(2, 1)
+        depth_sb[1, 1] = load_depth(1, 1)
+        w1_raw[2, 2] = load_w1(2, 2)
+
+        for s in range(2):
+            depth_sb[2, s] = load_depth(2, s)
+        w4_sb = keep.tile([P, 2, 2 * N], U8, name="w4_sb", align_bytes=64)
         nc.sync.dma_start(w4_sb[:].bitcast(I32), w4_words.rearrange("a p c -> p a c").bitcast(I32))
-        for t in range(1, PACK):
-            depth_sb[1, t] = load_depth(1, t)
         pos3_sb = load_list(pos3, "pos3_sb")
         pos4_sb = load_list(pos4, "pos4_sb")
         plots_sb = keep.tile([P, N_TILES, J], F32, name="plots_sb")
         nc.sync.dma_start(plots_sb[:], plots.rearrange("(n p) j -> p n j", p=P))
 
-        hs0 = [features(banks, 0, t) for t in range(PACK)]
+        z_dealt = keep.tile([P, 2, 2, M], BF16, name="z_dealt")
 
-        banks = [bank_tile(i) for i in range(PACK * HALVES)]
-        for a in range(K_PASSES):
-            w1_q = quantize(round_w1(w1_raw[1, a]), "w1_1%d" % a)
-            for t in range(PACK):
-                for half in range(HALVES):
-                    first_product(banks, w1_q, a, t, half)
-        z_q = [dam_maxima(hs0, "z0")]
-        hs1 = [features(banks, 1, t) for t in range(PACK)]
-        z_q.append(dam_maxima(hs1, "z1"))
+        def spare(name):
+            return ring.tile([P, M], F32, name=name, tag="spare", bufs=2)[:]
+
+        def narrow_tile(g, s, above, below):
+            pick_dams(hs[g, s], above, below)
+            nc.vector.tensor_tensor(z_dealt[:, g, s, :], above, below, ALU.max)
+
+        banks[1] = [bank_tile(4 + i) for i in range(4)]
+        first_pass(1, 0, banks[1])
+        hs = {(0, s): bounded(0, s) for s in range(2)}
+        times_depth(0, 0, hs[0, 0])
+        first_pass(1, 1, banks[1])
+        narrow_tile(0, 0, spare("above00"), reused[1, 1][:])
+        times_depth(0, 1, hs[0, 1])
+        first_pass(1, 2, banks[1])
+        for s in range(2, 4):
+            depth_sb[2, s] = load_depth(2, s)
+        for s in range(2):
+            hs[1, s] = bounded(1, s)
+        banks[2] = [bank_tile(i) for i in range(8)]
+        first_pass(2, 0, banks[2])
+        narrow_tile(0, 1, reused[1, 2][:], reused[2, 0][:, :M])
+        times_depth(1, 0, hs[1, 0])
+        first_pass(2, 1, banks[2])
+        narrow_tile(1, 0, spare("above10"), reused[2, 1][:, :M])
+        times_depth(1, 1, hs[1, 1])
+        first_pass(2, 2, banks[2])
+        narrow_tile(1, 1, reused[2, 2][:, :M], reused[2, 2][:, M:])
+        for s in range(PACK):
+            hs[2, s] = bounded(2, s)
+
+        z_rows = keep.tile([P, PACK, M], BF16, name="z_rows")
+        for g in range(2):
+            for e in range(2):
+                nc.sync.dma_start(z_rows[64 * g : 64 * (g + 1), 2 * e : 2 * e + 2, :], z_dealt[e:P:2, g, :, :])
+
+        pairs = keep.tile([P, PACK, 2, M], F32, name="pairs", align_bytes=64)
+        z_first = pairs[:, PACK - 1, :, :].rearrange("p side m -> p (side m)").bitcast(BF16)
+        nc.scalar.copy(
+            z_first.rearrange("p (c i t) -> p c t i", i=4, t=PACK),
+            z_rows[:].rearrange("p t (c i) -> p c t i", i=4),
+        )
+        for s in range(PACK):
+            times_depth(2, s, hs[2, s])
+            if s == PACK - 1:
+                z_q = [quantize(z_first, M, "z0")]
+            pick_dams(hs[2, s], pairs[:, s, 0, :], pairs[:, s, 1, :])
+        z = keep.tile([P, PACK * M], BF16, name="z", align_bytes=64)
+        z_codes = keep.tile([P, M], U32, name="z_codes", align_bytes=64)
+        z_scales = keep.tile([P, M], U8, name="z_scales", align_bytes=64)
+        parts = [slice(part * M // 2, (part + 1) * M // 2) for part in range(2)]
+        for cols in parts:
+            nc.vector.tensor_tensor(
+                z[:, PACK * cols.start : PACK * cols.stop].rearrange("p (c i t) -> p c t i", i=4, t=PACK),
+                pairs[:, :, 0, cols].rearrange("p t (c i) -> p c t i", i=4),
+                pairs[:, :, 1, cols].rearrange("p t (c i) -> p c t i", i=4),
+                ALU.max,
+            )
+        for cols in parts:
+            nc.vector.quantize_mx(
+                out=z_codes[:, cols].bitcast(FP8X4),
+                scales=z_scales[:, cols],
+                in_=z[:, PACK * cols.start : PACK * cols.stop],
+            )
+        z_q.append((z_codes, z_scales))
 
         def second_product(n):
             bank = bank_tile(n)
-            for b in range(H_PASSES):
+            whole = slice(0, M)
+            passes = [(0, whole)] + [(1, cols) for cols in (parts if n == 0 else [whole])]
+            for i, (b, cols) in enumerate(passes):
                 codes, scales = z_q[b]
                 nc.tensor.matmul_mx(
-                    out=bank[:],
+                    out=bank[:, cols],
                     lhsT=w4_sb[:, b, 2 * n * P : 2 * (n + 1) * P].bitcast(FP4X4),
                     lhsT_scale=w4_planes[:, b, n * P : (n + 1) * P],
-                    rhs=codes[:].bitcast(FP8X4),
-                    rhs_scale=scales[:],
-                    start=(b == 0),
-                    stop=(b == H_PASSES - 1),
+                    rhs=codes[:, cols].bitcast(FP8X4),
+                    rhs_scale=scales[:, cols],
+                    start=(i == 0),
+                    stop=(i == len(passes) - 1),
                 )
             y = keep.tile([P, M], F32, name="y%d" % n)
             nc.scalar.copy(y[:], bank[:])

@@ -33,6 +33,7 @@ def tile_list_bog_dam_contrast_kernel(
     with ExitStack() as ctx:
         keep = ctx.enter_context(tc.tile_pool(name="keep", bufs=1))
         ring = ctx.enter_context(tc.tile_pool(name="ring", bufs=1))
+        relay = ctx.enter_context(tc.tile_pool(name="relay", bufs=1))
         psum = ctx.enter_context(tc.psum_pool(name="psum", bufs=1))
 
         def load_list(ap, name):
@@ -42,7 +43,9 @@ def tile_list_bog_dam_contrast_kernel(
 
         def load_w1(g, a):
             first, tiles = GROUPS[g]
-            if tiles == PACK:
+            if (g, a) == (2, 0):
+                raw = relay.tile([P, PACK, tiles * P], F32, name="w1_wide0", offset=0)
+            elif tiles == PACK:
                 raw = ring.tile([P, PACK, tiles * P], F32, name="w1_wide", tag="big", bufs=K_PASSES)
             else:
                 raw = ring.tile([P, PACK, tiles * P], F32, name="w1_raw", tag="w1_raw", bufs=4)
@@ -96,7 +99,7 @@ def tile_list_bog_dam_contrast_kernel(
         nc.vector.memset(table_scales[:].bitcast(I32), 0)
         table.append(load_table(0))
         for q in range(4):
-            nc.gpsimd.dma_start(
+            nc.sync.dma_start(
                 table_scales[32 * q : 32 * q + 4 * K_PASSES, :].bitcast(I32),
                 tab_scales[:, 4 * q : 4 * q + 4, :].bitcast(I32),
             )
@@ -117,8 +120,8 @@ def tile_list_bog_dam_contrast_kernel(
         w1_raw[0, 0] = load_w1(0, 0)
         table.append(load_table(1))
         w1_raw[0, 1] = load_w1(0, 1)
-        w1_raw[0, 2] = load_w1(0, 2)
         table.append(load_table(2))
+        w1_raw[0, 2] = load_w1(0, 2)
         w1_raw[1, 0] = load_w1(1, 0)
         depth_sb[0, 0] = load_depth(0, 0)
         pos1_sb = load_list(pos1, "pos1_sb")
@@ -132,13 +135,13 @@ def tile_list_bog_dam_contrast_kernel(
                 picked[a][:, lo:hi], table[a][:].bitcast(U32).indirect(offs_sb[:, lo // 16 : hi // 16])
             )
 
-        def first_pass(g, a, banks):
+        def first_pass(g, a, banks, rounded=None):
             tiles = GROUPS[g][1]
-            codes, scales = quantize(round_w1(g, a, w1_raw[g, a]), tiles * P, "w1_%d%d" % (g, a))
             if g == 0:
-                pieces = HALVES if a == K_PASSES - 1 else 1
-                for piece in range(pieces):
-                    pick_words(a, piece * S // pieces, (piece + 1) * S // pieces)
+                pick_words(a, 0, S)
+            if rounded is None:
+                rounded = round_w1(g, a, w1_raw[g, a])
+            codes, scales = quantize(rounded, tiles * P, "w1_%d%d" % (g, a))
             for s in range(tiles):
                 for half in range(HALVES):
                     cols = slice(half * BANK, (half + 1) * BANK)
@@ -153,17 +156,20 @@ def tile_list_bog_dam_contrast_kernel(
                     )
 
         def bounded(g, s):
-            h = ring.tile([P, S], F32, name="h", tag="h", bufs=4)
+            if g == 1:
+                h = relay.tile([P, S], F32, name="h1%d" % s, offset=4 * S * s)
+            else:
+                h = ring.tile([P, S], F32, name="h", tag="h", bufs=4)
             for half in range(HALVES):
                 cols = slice(half * BANK, (half + 1) * BANK)
                 nc.scalar.activation(h[:, cols], banks[g][s * HALVES + half][:], ACT.Tanh, bias=bias[g][:, s : s + 1])
             return h
 
         def times_depth(g, s, h):
-            pieces = HALVES if (g, s) == (0, 0) else 1
+            pieces = HALVES if True else 1
             for piece in range(pieces):
                 cols = slice(piece * S // pieces, (piece + 1) * S // pieces)
-                nc.vector.tensor_tensor(h[:, cols], h[:, cols], depth_sb[g, s][:, cols], ALU.mult)
+                (nc.vector if (g, s) == (0, 0) or (g, s, piece) == (2, 0, 1) else nc.gpsimd).tensor_tensor(h[:, cols], h[:, cols], depth_sb[g, s][:, cols], ALU.mult)
 
         def pick_dams(h, above, below):
             nc.vector.tensor_copy(above, h[:].indirect(pos1_sb[:]))
@@ -180,8 +186,8 @@ def tile_list_bog_dam_contrast_kernel(
         w1_raw[2, 0] = load_w1(2, 0)
         depth_sb[1, 0] = load_depth(1, 0)
         w1_raw[2, 1] = load_w1(2, 1)
-        depth_sb[1, 1] = load_depth(1, 1)
         w1_raw[2, 2] = load_w1(2, 2)
+        depth_sb[1, 1] = load_depth(1, 1)
 
         for s in range(2):
             depth_sb[2, s] = load_depth(2, s)
@@ -211,10 +217,11 @@ def tile_list_bog_dam_contrast_kernel(
         first_pass(1, 2, banks[1])
         for s in range(2, 4):
             depth_sb[2, s] = load_depth(2, s)
+        rounded20 = round_w1(2, 0, w1_raw[2, 0])
         for s in range(2):
             hs[1, s] = bounded(1, s)
         banks[2] = [bank_tile(i) for i in range(8)]
-        first_pass(2, 0, banks[2])
+        first_pass(2, 0, banks[2], rounded20)
         narrow_tile(0, 1, reused[1, 2][:], reused[2, 0][:, :M])
         times_depth(1, 0, hs[1, 0])
         first_pass(2, 1, banks[2])
@@ -225,7 +232,8 @@ def tile_list_bog_dam_contrast_kernel(
         for s in range(PACK):
             hs[2, s] = bounded(2, s)
 
-        z_rows = keep.tile([P, PACK, M], BF16, name="z_rows")
+        times_depth(2, 0, hs[2, 0])
+        z_rows = depth_sb[2, 0][:].bitcast(BF16).rearrange("p (t m) -> p t m", t=PACK)
         for g in range(2):
             for e in range(2):
                 nc.sync.dma_start(z_rows[64 * g : 64 * (g + 1), 2 * e : 2 * e + 2, :], z_dealt[e:P:2, g, :, :])
@@ -234,10 +242,11 @@ def tile_list_bog_dam_contrast_kernel(
         z_first = pairs[:, PACK - 1, :, :].rearrange("p side m -> p (side m)").bitcast(BF16)
         nc.scalar.copy(
             z_first.rearrange("p (c i t) -> p c t i", i=4, t=PACK),
-            z_rows[:].rearrange("p t (c i) -> p c t i", i=4),
+            z_rows.rearrange("p t (c i) -> p c t i", i=4),
         )
         for s in range(PACK):
-            times_depth(2, s, hs[2, s])
+            if s > 0:
+                times_depth(2, s, hs[2, s])
             if s == PACK - 1:
                 z_q = [quantize(z_first, M, "z0")]
             pick_dams(hs[2, s], pairs[:, s, 0, :], pairs[:, s, 1, :])

@@ -73,10 +73,14 @@ def tile_list_bog_dam_contrast_kernel(
                 tile = ring.tile([P, tiles * PASS], BF16, name="w1_bf16", tag="w1_bf16", bufs=2, align_bytes=64)
                 rounded = tile[:]
             pair = PACK // tiles
-            nc.scalar.copy(
-                rounded.rearrange("p (s c i j) -> p c j i s", s=tiles, i=pair, j=PACK),
-                raw[:].rearrange("p j (c i s) -> p c j i s", s=tiles, i=pair),
-            )
+            lines = P // pair
+            to = rounded.rearrange("p (s c i j) -> p c j i s", s=tiles, i=pair, j=PACK)
+            fro = raw[:].rearrange("p j (c i s) -> p c j i s", s=tiles, i=pair)
+            if (g, a) in ((2, 1), (2, 2)):
+                nc.vector.tensor_copy(to[:, : lines // 2], fro[:, : lines // 2])
+                nc.scalar.copy(to[:, lines // 2 :], fro[:, lines // 2 :])
+            else:
+                nc.scalar.copy(to, fro)
             return rounded
 
         def quantize(values, width, name):
@@ -99,15 +103,10 @@ def tile_list_bog_dam_contrast_kernel(
         nc.vector.memset(table_scales[:].bitcast(I32), 0)
         table.append(load_table(0))
         for q in range(4):
-            nc.sync.dma_start(
+            nc.gpsimd.dma_start(
                 table_scales[32 * q : 32 * q + 4 * K_PASSES, :].bitcast(I32),
                 tab_scales[:, 4 * q : 4 * q + 4, :].bitcast(I32),
             )
-        bias = []
-        for g, (first, tiles) in enumerate(GROUPS):
-            tile = keep.tile([P, tiles], F32, name="bias%d" % g)
-            nc.gpsimd.dma_start(tile[:], b1[first : first + tiles * P].rearrange("(p s) -> p s", s=tiles))
-            bias.append(tile)
         w4_planes = keep.tile([P, 2, N], U8, name="w4_planes", align_bytes=64)
         nc.vector.memset(w4_planes[:].bitcast(I32), 0)
         for q in range(4):
@@ -120,6 +119,10 @@ def tile_list_bog_dam_contrast_kernel(
         w1_raw[0, 0] = load_w1(0, 0)
         table.append(load_table(1))
         w1_raw[0, 1] = load_w1(0, 1)
+        bias_narrow = keep.tile([P, 2, 2], F32, name="bias_narrow")
+        nc.sync.dma_start(bias_narrow[:], b1[:PASS].rearrange("(g p s) -> p g s", g=2, s=2))
+        bias_wide = keep.tile([P, PACK], F32, name="bias_wide")
+        bias = [bias_narrow[:, 0, :], bias_narrow[:, 1, :], bias_wide[:]]
         table.append(load_table(2))
         w1_raw[0, 2] = load_w1(0, 2)
         w1_raw[1, 0] = load_w1(1, 0)
@@ -189,6 +192,7 @@ def tile_list_bog_dam_contrast_kernel(
         w1_raw[2, 2] = load_w1(2, 2)
         depth_sb[1, 1] = load_depth(1, 1)
 
+        nc.sync.dma_start(bias_wide[:], b1[PASS:].rearrange("(p s) -> p s", s=PACK))
         for s in range(2):
             depth_sb[2, s] = load_depth(2, s)
         w4_sb = keep.tile([P, 2, 2 * N], U8, name="w4_sb", align_bytes=64)
@@ -270,22 +274,21 @@ def tile_list_bog_dam_contrast_kernel(
         z_q.append((z_codes, z_scales))
 
         def second_product(n):
-            bank = bank_tile(n)
-            whole = slice(0, M)
-            passes = [(0, whole)] + [(1, cols) for cols in (parts if n == 0 else [whole])]
-            for i, (b, cols) in enumerate(passes):
-                codes, scales = z_q[b]
-                nc.tensor.matmul_mx(
-                    out=bank[:, cols],
-                    lhsT=w4_sb[:, b, 2 * n * P : 2 * (n + 1) * P].bitcast(FP4X4),
-                    lhsT_scale=w4_planes[:, b, n * P : (n + 1) * P],
-                    rhs=codes[:, cols].bitcast(FP8X4),
-                    rhs_scale=scales[:, cols],
-                    start=(i == 0),
-                    stop=(i == len(passes) - 1),
-                )
             y = keep.tile([P, M], F32, name="y%d" % n)
-            nc.scalar.copy(y[:], bank[:])
+            for i, cols in enumerate(parts if n == 0 else [slice(0, M)]):
+                bank = bank_tile(N_TILES + i if n == 0 else n)
+                for b in range(2):
+                    codes, scales = z_q[b]
+                    nc.tensor.matmul_mx(
+                        out=bank[:, cols],
+                        lhsT=w4_sb[:, b, 2 * n * P : 2 * (n + 1) * P].bitcast(FP4X4),
+                        lhsT_scale=w4_planes[:, b, n * P : (n + 1) * P],
+                        rhs=codes[:, cols].bitcast(FP8X4),
+                        rhs_scale=scales[:, cols],
+                        start=(b == 0),
+                        stop=(b == 1),
+                    )
+                nc.scalar.copy(y[:, cols], bank[:, cols])
             return y
 
         ahead = 2

from contextlib import ExitStack

import concourse.mybir as mybir

K, T, S, H, M, N, J = 1536, 4096, 1024, 1024, 512, 768, 256
FLOPS = 2 * K * H * S + 2 * H * N * M

F32 = mybir.dt.float32
BF16 = mybir.dt.bfloat16
I32 = mybir.dt.int32
U32 = mybir.dt.uint32
U16 = mybir.dt.uint16
U8 = mybir.dt.uint8
FP8X4 = mybir.dt.float8_e4m3fn_x4
FP4X4 = mybir.dt.float4_e2m1fn_x4
ALU = mybir.AluOpType
ACT = mybir.ActivationFunctionType

P = 128
PACK = 4
PASS = P * PACK
BANK = 512
K_PASSES = K // PASS
N_TILES = N // P
HALVES = S // BANK
GROUPS = ((0, 2), (256, 2), (512, 4))


def tile_list_bog_dam_contrast_kernel(
    tc, tab_words, tab_scales, offs, pos1, pos2, pos3, pos4, w1, b1, depth, w4_words, w4_scales, plots, out
):
    nc = tc.nc
    with ExitStack() as ctx:
        keep = ctx.enter_context(tc.tile_pool(name="keep", bufs=1))
        ring = ctx.enter_context(tc.tile_pool(name="ring", bufs=1))
        relay = ctx.enter_context(tc.tile_pool(name="relay", bufs=1))
        psum = ctx.enter_context(tc.psum_pool(name="psum", bufs=1))

        def load_list(ap, name):
            tile = keep.tile([P, ap.shape[1]], U16, name=name)
            nc.sync.dma_start(tile[:], ap)
            return tile

        def load_w1(g, a):
            first, tiles = GROUPS[g]
            if (g, a) == (2, 0):
                raw = relay.tile([P, PACK, tiles * P], F32, name="w1_wide0", offset=0)
            elif tiles == PACK:
                raw = ring.tile([P, PACK, tiles * P], F32, name="w1_wide", tag="big", bufs=K_PASSES)
            else:
                raw = ring.tile([P, PACK, tiles * P], F32, name="w1_raw", tag="w1_raw", bufs=4)
            rows = w1[a * PASS : (a + 1) * PASS, first : first + tiles * P]
            nc.sync.dma_start(raw[:], rows.rearrange("(p j) c -> p j c", j=PACK))
            return raw

        def load_table(a):
            tile = ring.tile([P, T], I32, name="table", tag="big", bufs=K_PASSES)
            nc.sync.dma_start(tile[:], tab_words[a].rearrange("p t i -> p (t i)").bitcast(I32))
            return tile

        def load_depth(g, s):
            first, tiles = GROUPS[g]
            tile = ring.tile([P, S], F32, name="depth_sb", tag="depth_sb", bufs=6, align_bytes=64)
            rows = depth[first : first + tiles * P, :].rearrange("(p s) j -> p s j", s=tiles)
            nc.sync.dma_start(tile[:], rows[:, s, :])
            return tile

        def round_w1(g, a, raw):
            tiles = GROUPS[g][1]
            if (g, a) in reused:
                rounded = reused[g, a][:].bitcast(BF16)
            else:
                tile = ring.tile([P, tiles * PASS], BF16, name="w1_bf16", tag="w1_bf16", bufs=2, align_bytes=64)
                rounded = tile[:]
            pair = PACK // tiles
            lines = P // pair
            to = rounded.rearrange("p (s c i j) -> p c j i s", s=tiles, i=pair, j=PACK)
            fro = raw[:].rearrange("p j (c i s) -> p c j i s", s=tiles, i=pair)
            if (g, a) in ((2, 1), (2, 2)):
                nc.vector.tensor_copy(to[:, : lines // 2], fro[:, : lines // 2])
                nc.scalar.copy(to[:, lines // 2 :], fro[:, lines // 2 :])
            else:
                nc.scalar.copy(to, fro)
            return rounded

        def quantize(values, width, name):
            codes = keep.tile([P, width], U32, name=name + "_codes", align_bytes=64)
            scales = keep.tile([P, width], U8, name=name + "_scales", align_bytes=64)
            nc.vector.quantize_mx(out=codes[:].bitcast(FP8X4), scales=scales[:], in_=values)
            return codes, scales

        def bank_tile(i):
            return psum.tile([P, BANK], F32, name="bank%d" % i, tag="bank%d" % i)

        reused = {
            (g, a): keep.tile([P, GROUPS[g][1] * PASS // 2], F32, name="reused%d%d" % (g, a), align_bytes=64)
            for g, a in ((1, 1), (1, 2), (2, 0), (2, 1), (2, 2))
        }
        w1_raw = {}
        table = []
        depth_sb = {}
        table_scales = keep.tile([P, T], U8, name="table_scales")
        nc.vector.memset(table_scales[:].bitcast(I32), 0)
        table.append(load_table(0))
        for q in range(4):
            nc.gpsimd.dma_start(
                table_scales[32 * q : 32 * q + 4 * K_PASSES, :].bitcast(I32),
                tab_scales[:, 4 * q : 4 * q + 4, :].bitcast(I32),
            )
        w4_planes = keep.tile([P, 2, N], U8, name="w4_planes", align_bytes=64)
        nc.vector.memset(w4_planes[:].bitcast(I32), 0)
        for q in range(4):
            nc.gpsimd.dma_start(
                w4_planes[32 * q : 32 * q + 4, :, :].bitcast(I32),
                w4_scales[:, 4 * q : 4 * q + 4, :].rearrange("a r c -> r a c").bitcast(I32),
            )

        offs_sb = load_list(offs, "offs_sb")
        w1_raw[0, 0] = load_w1(0, 0)
        table.append(load_table(1))
        w1_raw[0, 1] = load_w1(0, 1)
        bias_narrow = keep.tile([P, 2, 2], F32, name="bias_narrow")
        nc.sync.dma_start(bias_narrow[:], b1[:PASS].rearrange("(g p s) -> p g s", g=2, s=2))
        bias_wide = keep.tile([P, PACK], F32, name="bias_wide")
        bias = [bias_narrow[:, 0, :], bias_narrow[:, 1, :], bias_wide[:]]
        table.append(load_table(2))
        w1_raw[0, 2] = load_w1(0, 2)
        w1_raw[1, 0] = load_w1(1, 0)
        depth_sb[0, 0] = load_depth(0, 0)
        pos1_sb = load_list(pos1, "pos1_sb")
        pos2_sb = load_list(pos2, "pos2_sb")

        picked_scales = keep.tile([P, S], U8, name="picked_scales", align_bytes=64)
        picked = [keep.tile([P, S], U32, name="picked%d" % a, align_bytes=64) for a in range(K_PASSES)]

        def pick_words(a, lo, hi):
            nc.vector.tensor_copy(
                picked[a][:, lo:hi], table[a][:].bitcast(U32).indirect(offs_sb[:, lo // 16 : hi // 16])
            )

        def first_pass(g, a, banks, rounded=None):
            tiles = GROUPS[g][1]
            if g == 0:
                pick_words(a, 0, S)
            if rounded is None:
                rounded = round_w1(g, a, w1_raw[g, a])
            codes, scales = quantize(rounded, tiles * P, "w1_%d%d" % (g, a))
            for s in range(tiles):
                for half in range(HALVES):
                    cols = slice(half * BANK, (half + 1) * BANK)
                    nc.tensor.matmul_mx(
                        out=banks[s * HALVES + half][:],
                        lhsT=codes[:, s * P : (s + 1) * P].bitcast(FP8X4),
                        lhsT_scale=scales[:, s * P : (s + 1) * P],
                        rhs=picked[a][:, cols].bitcast(FP8X4),
                        rhs_scale=picked_scales[4 * a : P, cols],
                        start=(a == 0),
                        stop=(a == K_PASSES - 1),
                    )

        def bounded(g, s):
            if g == 1:
                h = relay.tile([P, S], F32, name="h1%d" % s, offset=4 * S * s)
            else:
                h = ring.tile([P, S], F32, name="h", tag="h", bufs=4)
            for half in range(HALVES):
                cols = slice(half * BANK, (half + 1) * BANK)
                nc.scalar.activation(h[:, cols], banks[g][s * HALVES + half][:], ACT.Tanh, bias=bias[g][:, s : s + 1])
            return h

        def times_depth(g, s, h):
            pieces = HALVES if True else 1
            for piece in range(pieces):
                cols = slice(piece * S // pieces, (piece + 1) * S // pieces)
                (nc.vector if (g, s) == (0, 0) or (g, s, piece) == (2, 0, 1) else nc.gpsimd).tensor_tensor(h[:, cols], h[:, cols], depth_sb[g, s][:, cols], ALU.mult)

        def pick_dams(h, above, below):
            nc.vector.tensor_copy(above, h[:].indirect(pos1_sb[:]))
            nc.vector.tensor_copy(below, h[:].indirect(pos2_sb[:]))

        nc.vector.tensor_copy(picked_scales[:], table_scales[:].indirect(offs_sb[:]))
        banks = {0: [bank_tile(i) for i in range(4)]}
        for a in range(K_PASSES):
            first_pass(0, a, banks[0])

        w1_raw[1, 1] = load_w1(1, 1)
        w1_raw[1, 2] = load_w1(1, 2)
        depth_sb[0, 1] = load_depth(0, 1)
        w1_raw[2, 0] = load_w1(2, 0)
        depth_sb[1, 0] = load_depth(1, 0)
        w1_raw[2, 1] = load_w1(2, 1)
        w1_raw[2, 2] = load_w1(2, 2)
        depth_sb[1, 1] = load_depth(1, 1)

        nc.sync.dma_start(bias_wide[:], b1[PASS:].rearrange("(p s) -> p s", s=PACK))
        for s in range(2):
            depth_sb[2, s] = load_depth(2, s)
        w4_sb = keep.tile([P, 2, 2 * N], U8, name="w4_sb", align_bytes=64)
        nc.sync.dma_start(w4_sb[:].bitcast(I32), w4_words.rearrange("a p c -> p a c").bitcast(I32))
        pos3_sb = load_list(pos3, "pos3_sb")
        pos4_sb = load_list(pos4, "pos4_sb")
        plots_sb = keep.tile([P, N_TILES, J], F32, name="plots_sb")
        nc.sync.dma_start(plots_sb[:], plots.rearrange("(n p) j -> p n j", p=P))

        z_dealt = keep.tile([P, 2, 2, M], BF16, name="z_dealt")

        def spare(name):
            return ring.tile([P, M], F32, name=name, tag="spare", bufs=2)[:]

        def narrow_tile(g, s, above, below):
            pick_dams(hs[g, s], above, below)
            nc.vector.tensor_tensor(z_dealt[:, g, s, :], above, below, ALU.max)

        banks[1] = [bank_tile(4 + i) for i in range(4)]
        first_pass(1, 0, banks[1])
        hs = {(0, s): bounded(0, s) for s in range(2)}
        times_depth(0, 0, hs[0, 0])
        first_pass(1, 1, banks[1])
        narrow_tile(0, 0, spare("above00"), reused[1, 1][:])
        times_depth(0, 1, hs[0, 1])
        first_pass(1, 2, banks[1])
        for s in range(2, 4):
            depth_sb[2, s] = load_depth(2, s)
        rounded20 = round_w1(2, 0, w1_raw[2, 0])
        for s in range(2):
            hs[1, s] = bounded(1, s)
        banks[2] = [bank_tile(i) for i in range(8)]
        first_pass(2, 0, banks[2], rounded20)
        narrow_tile(0, 1, reused[1, 2][:], reused[2, 0][:, :M])
        times_depth(1, 0, hs[1, 0])
        first_pass(2, 1, banks[2])
        narrow_tile(1, 0, spare("above10"), reused[2, 1][:, :M])
        times_depth(1, 1, hs[1, 1])
        first_pass(2, 2, banks[2])
        narrow_tile(1, 1, reused[2, 2][:, :M], reused[2, 2][:, M:])
        for s in range(PACK):
            hs[2, s] = bounded(2, s)

        times_depth(2, 0, hs[2, 0])
        z_rows = depth_sb[2, 0][:].bitcast(BF16).rearrange("p (t m) -> p t m", t=PACK)
        for g in range(2):
            for e in range(2):
                nc.sync.dma_start(z_rows[64 * g : 64 * (g + 1), 2 * e : 2 * e + 2, :], z_dealt[e:P:2, g, :, :])

        pairs = keep.tile([P, PACK, 2, M], F32, name="pairs", align_bytes=64)
        z_first = pairs[:, PACK - 1, :, :].rearrange("p side m -> p (side m)").bitcast(BF16)
        nc.scalar.copy(
            z_first.rearrange("p (c i t) -> p c t i", i=4, t=PACK),
            z_rows.rearrange("p t (c i) -> p c t i", i=4),
        )
        for s in range(PACK):
            if s > 0:
                times_depth(2, s, hs[2, s])
            if s == PACK - 1:
                z_q = [quantize(z_first, M, "z0")]
            pick_dams(hs[2, s], pairs[:, s, 0, :], pairs[:, s, 1, :])
        z = keep.tile([P, PACK * M], BF16, name="z", align_bytes=64)
        z_codes = keep.tile([P, M], U32, name="z_codes", align_bytes=64)
        z_scales = keep.tile([P, M], U8, name="z_scales", align_bytes=64)
        parts = [slice(part * M // 2, (part + 1) * M // 2) for part in range(2)]
        for cols in parts:
            nc.vector.tensor_tensor(
                z[:, PACK * cols.start : PACK * cols.stop].rearrange("p (c i t) -> p c t i", i=4, t=PACK),
                pairs[:, :, 0, cols].rearrange("p t (c i) -> p c t i", i=4),
                pairs[:, :, 1, cols].rearrange("p t (c i) -> p c t i", i=4),
                ALU.max,
            )
        for cols in parts:
            nc.vector.quantize_mx(
                out=z_codes[:, cols].bitcast(FP8X4),
                scales=z_scales[:, cols],
                in_=z[:, PACK * cols.start : PACK * cols.stop],
            )
        z_q.append((z_codes, z_scales))

        def second_product(n):
            y = keep.tile([P, M], F32, name="y%d" % n)
            for i, cols in enumerate(parts if n == 0 else [slice(0, M)]):
                bank = bank_tile(N_TILES + i if n == 0 else n)
                for b in range(2):
                    codes, scales = z_q[b]
                    nc.tensor.matmul_mx(
                        out=bank[:, cols],
                        lhsT=w4_sb[:, b, 2 * n * P : 2 * (n + 1) * P].bitcast(FP4X4),
                        lhsT_scale=w4_planes[:, b, n * P : (n + 1) * P],
                        rhs=codes[:, cols].bitcast(FP8X4),
                        rhs_scale=scales[:, cols],
                        start=(b == 0),
                        stop=(b == 1),
                    )
                nc.scalar.copy(y[:, cols], bank[:, cols])
            return y

        ahead = 2
        ys = [second_product(n) for n in range(ahead)]
        for n in range(N_TILES):
            if n + ahead < N_TILES:
                ys.append(second_product(n + ahead))
            one = ring.tile([P, J], F32, name="one", tag="one", bufs=2)
            nc.vector.tensor_copy(one[:], ys[n][:].indirect(pos3_sb[:]))
            gap = ring.tile([P, J], F32, name="gap", tag="gap", bufs=2)
            nc.vector.tensor_tensor(gap[:], ys[n][:].indirect(pos4_sb[:]), one[:], ALU.subtract)
            nc.scalar.activation(gap[:], gap[:], ACT.Abs)
            result = ring.tile([P, J], F32, name="result", tag="result", bufs=N_TILES)
            nc.vector.tensor_tensor(result[:], gap[:], plots_sb[:, n, :], ALU.mult)
            nc.sync.dma_start(out[n * P : (n + 1) * P, :], result[:])
